import numpy as np
import ml_dtypes


def mxq(x, axis, fmt="e4m3"):
    dtype, down = {"e4m3": (ml_dtypes.float8_e4m3fn, 7), "e5m2": (ml_dtypes.float8_e5m2, 14)}[fmt]
    v = np.moveaxis(np.asarray(x, np.float32).astype(ml_dtypes.bfloat16).astype(np.float64), axis, -1)
    blocks = v.reshape(v.shape[:-1] + (-1, 32))
    amax = np.abs(blocks).max(-1, keepdims=True)
    byte = np.maximum(np.where(amax > 0, np.frexp(amax)[1] - 1 + 127, 0) - down, 1)
    scale = np.exp2(byte - 127.0)
    codes = (blocks / scale).astype(np.float32).astype(dtype).astype(np.float64)
    return np.moveaxis((codes * scale).reshape(v.shape), -1, axis)


WIDE = False


def mx_kscale(k):
    if not WIDE:
        return np.ones(k)
    levels = np.array([10, -10, 5, -5, 0])
    if k % 512:
        return np.exp2(np.random.permutation(np.resize(levels, k // 32))).repeat(32)
    a = np.empty((k // 512, 16))
    for p in range(k // 512):
        a[p, :8] = np.random.permutation(np.resize(levels, 8))
        for g in range(8):
            far = levels[np.abs(levels - a[p, g]) >= 10]
            a[p, g + 8] = far[np.random.randint(len(far))]
    return np.exp2(a.ravel()).repeat(32)


def f64(x):
    return np.asarray(x).astype(np.float64)


def striped(idx):
    return np.tile(idx.reshape(-1, 16).T, (8, 1)).astype(np.uint16)


def unstriped(offs):
    return offs[:16].T.reshape(-1).astype(np.int64)


E2M1 = np.array([0.0, 0.5, 1.0, 1.5, 2.0, 3.0, 4.0, 6.0, -0.0, -0.5, -1.0, -1.5, -2.0, -3.0, -4.0, -6.0])


def pack_weight(w, fmt):
    k, n = w.shape
    w = f64(np.asarray(w, np.float32).astype(ml_dtypes.bfloat16)).reshape(k // 32, 32, n)
    amax = np.abs(w).max(1)
    if fmt == "e4m3":
        byte = np.frexp(amax)[1] - 1 + 127 - 7
    else:
        mant, ex = np.frexp(amax / 6.0)
        byte = np.where(mant > 0.5, ex, ex - 1) + 127
    byte = np.clip(np.where(amax > 0, byte, 1), 1, 254)
    scaled = (w * np.exp2(127.0 - byte)[:, None, :]).reshape(k, n).astype(np.float32)
    by_word = np.ascontiguousarray(scaled.reshape(k // 512, 128, 4, n).transpose(0, 1, 3, 2))
    if fmt == "e4m3":
        words = by_word.astype(ml_dtypes.float8_e4m3fn).view(np.uint8)
    else:
        c = by_word.astype(ml_dtypes.float4_e2m1fn).view(np.uint8) & 0xF
        words = (c[..., 0::2] | (c[..., 1::2] << 4)).reshape(k // 512, 128, 2 * n)
    return np.ascontiguousarray(words), np.ascontiguousarray(byte.astype(np.uint8).reshape(k // 512, 16, n))


def unpack_weight(words, scales, fmt):
    g, _, n = scales.shape
    words = np.ascontiguousarray(words).reshape(g, 128, n, -1)
    if fmt == "e4m3":
        vals = words.view(ml_dtypes.float8_e4m3fn).astype(np.float64)
    else:
        nib = np.empty((g, 128, n, 4), np.uint8)
        nib[..., 0::2] = words & 0xF
        nib[..., 1::2] = words >> 4
        vals = E2M1[nib]
    vals = vals * np.repeat(np.exp2(scales.astype(np.float64) - 127.0), 8, axis=1)[..., None]
    return vals.transpose(0, 1, 3, 2).reshape(g * 512, n)


def gelu(v):
    return 0.5 * v * (1.0 + np.tanh(np.sqrt(2.0 / np.pi) * (v + 0.044715 * v**3)))


def striped8(idx):
    return np.concatenate([v.reshape(-1, 16).T for v in idx]).astype(np.uint16)


def unstriped8(offs):
    return np.stack([offs[16 * g:16 * g + 16].T.reshape(-1) for g in range(8)]).astype(np.int64)


def runs(v, idx8):
    k = np.arange(v.shape[0])
    return v[k[:, None], idx8[k % 512 // 64]]


K, K2, H, N, T, S, T2 = 1024, 512, 1024, 512, 2048, 1024, 2048

def setup_inputs():
    n = np.random.standard_normal
    s = mx_kscale(K)[:, None]
    s2 = mx_kscale(K2)[:, None]
    u = mx_kscale(H)[:, None]
    tab_words, tab_scales = pack_weight(n((K, T)) * s, "e4m3")
    tab2_words, tab2_scales = pack_weight(n((K2, T)) * s2, "e4m3")
    w2_words, w2_scales = pack_weight(1.6 * n((K2, H)) / np.sqrt(K2) / s2, "e2m1")
    return {
        "tab_words": tab_words, "tab_scales": tab_scales,
        "tab2_words": tab2_words, "tab2_scales": tab2_scales,
        "offs": striped8(np.stack([np.random.permutation(T)[:S] for _ in range(8)])),
        "offs2": striped(np.random.permutation(T)[:S]),
        "offs3": striped(np.random.permutation(T2)[:S]),
        "w1": (n((K, H)) / np.sqrt(K) / s * u.T).astype(np.float32),
        "w2_words": w2_words, "w2_scales": w2_scales,
        "w3": (1.5 * n((H, N)) / np.sqrt(H) / u).astype(np.float32),
        "wgo": np.exp(0.3 * n((128, S))).astype(np.float32),
        "page1": n((N, T2)).astype(np.float32),
    }

def reference(tab_words, tab_scales, tab2_words, tab2_scales, offs, offs2, offs3,
              w1, w2_words, w2_scales, w3, wgo, page1):
    v = runs(unpack_weight(tab_words, tab_scales, "e4m3"), unstriped8(offs))
    v2 = unpack_weight(tab2_words, tab2_scales, "e4m3")[:, unstriped(offs2)]
    step = mxq(f64(w1), 0, "e4m3").T @ v
    surf = unpack_weight(w2_words, w2_scales, "e2m1").T @ v2
    h = step / np.sqrt(1.0 + np.square(surf))
    y = mxq(f64(w3), 0, "e4m3").T @ mxq(h, 0, "e4m3")
    out = f64(page1).copy()
    out[:, unstriped(offs3)] = np.tile(f64(wgo), (N // 128, 1)) * y
    return out

from contextlib import ExitStack

import concourse.mybir as mybir

K, K2, H, N, T, S = 1024, 512, 1024, 512, 2048, 1024
FLOPS = 2 * S * (K * H + K2 * H + H * N)

F32 = mybir.dt.float32
BF16 = mybir.dt.bfloat16
I32 = mybir.dt.int32
U32 = mybir.dt.uint32
U16 = mybir.dt.uint16
U8 = mybir.dt.uint8
FP8X4 = mybir.dt.float8_e4m3fn_x4
FP4X4 = mybir.dt.float4_e2m1fn_x4
ACT = mybir.ActivationFunctionType
MULT = mybir.AluOpType.mult

P = 128
PACK = 4
PASS = P * PACK
CUES = 128
HALF = 512
LIST = 16
PLANE_STEP = 8


def tile_list_footstep_floor_fit_kernel(
    tc, tab_words, tab_scales, tab2_words, tab2_scales, offs, offs2, offs3,
    w1, w2_words, w2_scales, w3, wgo, page1, out,
):
    nc = tc.nc
    with ExitStack() as ctx:
        keep = ctx.enter_context(tc.tile_pool(name="keep", bufs=1))
        ring = ctx.enter_context(tc.tile_pool(name="ring", bufs=2))
        psum = ctx.enter_context(tc.psum_pool(name="psum", bufs=2))

        def held(shape, dtype, name):
            return keep.tile(shape, dtype, name=name, align_bytes=64)

        idx = held([P, S // LIST], U16, "idx")
        idx2 = held([P, S // LIST], U16, "idx2")
        idx3 = held([P, S // LIST], U16, "idx3")
        tab_w = [held([P, T], U32, f"tab_w{a}") for a in range(2)]
        tab_s = held([P, T], U8, "tab_s")
        tab2_w = held([P, T], U32, "tab2_w")
        tab2_s = held([P, T], U8, "tab2_s")
        w2_raw = held([P, 2 * H], U8, "w2_raw")
        w2_raw_s = held([P, H], U8, "w2_raw_s")
        w1_raw = {(a, b): held([P, PACK, PASS], F32, f"w1_raw{a}{b}") for a in range(2) for b in range(2)}
        w3_raw = [held([P, PACK, N], F32, f"w3_raw{b}") for b in range(2)]
        gate = held([P, S], F32, "gate")
        pages = [held([P, T], F32, f"page{n}") for n in range(N // P)]

        nc.gpsimd.memset(tab2_s[:].bitcast(I32), 0)
        nc.vector.memset(w2_raw_s[:].bitcast(I32), 0)
        nc.vector.memset(tab_s[:].bitcast(I32), 0)

        def load_words(tile, words):
            nc.sync.dma_start(tile[:].bitcast(I32), words.rearrange("p t i -> p (t i)").bitcast(I32))

        def load_w1(a, b):
            rows = w1[a * PASS:(a + 1) * PASS, b * PASS:(b + 1) * PASS]
            nc.sync.dma_start(w1_raw[a, b][:], rows.rearrange("(p j) c -> p j c", j=PACK))

        def load_plane(tile, rows):
            for d in range(4):
                nc.sync.dma_start(tile[:].bitcast(I32)[32 * d:32 * d + 4, :], rows.bitcast(I32)[4 * d:4 * d + 4, :])

        nc.sync.dma_start(idx2[:], offs2)
        nc.sync.dma_start(idx[:], offs)
        nc.sync.dma_start(w2_raw[:].bitcast(I32), w2_words[0].bitcast(I32))
        load_plane(tab2_s, tab2_scales[0])
        load_words(tab2_w, tab2_words[0])
        load_plane(w2_raw_s, w2_scales[0])
        tab_rows = tab_scales.bitcast(I32).rearrange("a (g e) t -> e g a t", e=2)
        for e in range(2):
            nc.sync.dma_start(tab_s[:].bitcast(I32)[e:P:PLANE_STEP, :], tab_rows[e])
        load_w1(0, 0)
        load_words(tab_w[0], tab_words[0])
        load_w1(1, 0)
        load_words(tab_w[1], tab_words[1])
        load_w1(0, 1)
        load_w1(1, 1)
        for b in range(2):
            rows = w3[b * PASS:(b + 1) * PASS, :].rearrange("(u t i) n -> t u i n", t=PACK, i=4)
            for t in range(PACK):
                nc.sync.dma_start(w3_raw[b][:, t, :], rows[t])
        nc.sync.dma_start(idx3[:], offs3)
        nc.sync.dma_start(gate[:], wgo)
        for n in range(N // P):
            nc.sync.dma_start(pages[n][:], page1[n * P:(n + 1) * P, :])

        v2_c = held([P, S], U32, "v2_c")
        v2_s = held([P, S], U8, "v2_s")

        def pick(dst, window, offsets, half):
            entries = offsets[:, half * HALF // LIST:(half + 1) * HALF // LIST]
            nc.vector.tensor_copy(dst[:, half * HALF:(half + 1) * HALF], window[:].indirect(entries))

        pick(v2_s, tab2_s, idx2, 0)
        pick(v2_c, tab2_w, idx2, 0)

        w2_c = held([P, 2 * H], U8, "w2_c")
        w2_s = held([P, H], U8, "w2_s")
        nc.vector.tensor_copy(
            w2_c[:].bitcast(I32).rearrange("p (b t u w) -> p b t u w", b=2, t=PACK, w=2),
            w2_raw[:].bitcast(I32).rearrange("p (b u t w) -> p b t u w", b=2, t=PACK, w=2),
        )
        nc.vector.tensor_copy(
            w2_s[:].bitcast(I32).rearrange("p (b t u) -> p b t u", b=2, t=PACK),
            w2_raw_s[:].bitcast(I32).rearrange("p (b u t) -> p b t u", b=2, t=PACK),
        )

        v_picked_s = held([P, S], U8, "v_picked_s")
        v_s = held([P, S], U8, "v_s")
        nc.vector.tensor_copy(v_picked_s[:], tab_s[:].indirect(idx[:]))
        nc.vector.tensor_copy(v_s[:].bitcast(I32), v_picked_s[:].bitcast(I32))
        for a in range(2):
            for e in range(2):
                row = PLANE_STEP * a + e
                nc.gpsimd.dma_start(v_s[:].bitcast(I32)[row + 2:P:32, :], v_picked_s[:].bitcast(I32)[row + 16:P:32, :])

        v_c = [held([P, S], U32, f"v_c{a}") for a in range(2)]
        w1_c, w1_s, w3_c, w3_s = {}, {}, {}, {}

        def cast(engine, dst, src):
            if engine == "scalar":
                nc.scalar.copy(dst, src)
            else:
                nc.vector.tensor_copy(dst, src)

        def quantise(rounded, name):
            codes = held([P, PASS], U32, name + "_c")
            scales = held([P, PASS], U8, name + "_s")
            nc.vector.quantize_mx(out=codes[:].bitcast(FP8X4), scales=scales[:], in_=rounded[:])
            return codes, scales

        def prepare_w1(a, b, engine):
            rounded = ring.tile([P, PACK * PASS], BF16, name="w_rounded", align_bytes=64, bufs=3)
            cast(
                engine,
                rounded[:].rearrange("p (t u i j) -> p u t j i", t=PACK, i=4, j=PACK),
                w1_raw[a, b][:].rearrange("p j (u t i) -> p u t j i", t=PACK, i=4),
            )
            w1_c[a, b], w1_s[a, b] = quantise(rounded, f"w1q{a}{b}")

        def prepare_w3(b, engine):
            rounded = ring.tile([P, PACK * N], BF16, name="w_rounded", align_bytes=64, bufs=3)
            cast(
                engine,
                rounded[:].rearrange("p (c i t) -> p c t i", i=4, t=PACK),
                w3_raw[b][:].rearrange("p t (c i) -> p c t i", i=4),
            )
            w3_c[b], w3_s[b] = quantise(rounded, f"w3q{b}")

        prepare_w1(0, 0, "scalar")
        nc.vector.tensor_copy(v_c[0][:], tab_w[0][:].indirect(idx[:]))
        prepare_w1(1, 0, "scalar")
        nc.vector.tensor_copy(v_c[1][:], tab_w[1][:].indirect(idx[:]))
        pick(v2_s, tab2_s, idx2, 1)
        pick(v2_c, tab2_w, idx2, 1)
        prepare_w1(0, 1, "vector")
        prepare_w1(1, 1, "vector")
        prepare_w3(0, "scalar")
        prepare_w3(1, "scalar")

        def damping(b, c):
            cues = slice(c * CUES, (c + 1) * CUES)
            surf = psum.tile([P, PACK, CUES], F32, name="surf", bufs=3)
            for t in range(PACK):
                col = (b * PACK + t) * P
                nc.tensor.matmul_mx(
                    out=surf[:, t, :],
                    lhsT=w2_c[:, 2 * col:2 * (col + P)].bitcast(FP4X4), lhsT_scale=w2_s[:, col:col + P],
                    rhs=v2_c[:, cues].bitcast(FP8X4), rhs_scale=v2_s[:, cues],
                    start=True, stop=True,
                )
            squared = ring.tile([P, CUES, PACK], F32, name="squared")
            nc.scalar.activation(squared[:], surf[:].rearrange("p t j -> p j t"), ACT.Square)
            factor = ring.tile([P, CUES, PACK], F32, name="factor", bufs=12)
            nc.scalar.activation(factor[:], squared[:], ACT.Abs_reciprocal_sqrt, bias=1.0)
            return factor

        def hidden(b, half, factors):
            rounded = ring.tile([P, PACK * HALF], BF16, name="h_rounded", align_bytes=64)
            for q, factor in enumerate(factors):
                c = half * (HALF // CUES) + q
                cues = slice(c * CUES, (c + 1) * CUES)
                step = psum.tile([P, PACK, CUES], F32, name="step", bufs=3)
                for t in range(PACK):
                    cols = slice(t * P, (t + 1) * P)
                    for a in range(2):
                        nc.tensor.matmul_mx(
                            out=step[:, t, :],
                            lhsT=w1_c[a, b][:, cols].bitcast(FP8X4), lhsT_scale=w1_s[a, b][:, cols],
                            rhs=v_c[a][:, cues].bitcast(FP8X4), rhs_scale=v_s[PLANE_STEP * a:P, cues],
                            start=(a == 0), stop=(a == 1),
                        )
                part = rounded[:, q * PACK * CUES:(q + 1) * PACK * CUES]
                nc.vector.tensor_tensor(
                    part.rearrange("p (j t) -> p j t", t=PACK), step[:].rearrange("p t j -> p j t"), factor[:], MULT
                )
            return quantise(rounded, f"h{b}{half}")

        def place(half, n, h):
            y_bank = psum.tile([P, HALF], F32, name="y_bank")
            cols = slice(n * P, (n + 1) * P)
            for b in range(2):
                nc.tensor.matmul_mx(
                    out=y_bank[:],
                    lhsT=w3_c[b][:, cols].bitcast(FP8X4), lhsT_scale=w3_s[b][:, cols],
                    rhs=h[b][0][:].bitcast(FP8X4), rhs_scale=h[b][1][:],
                    start=(b == 0), stop=(b == 1),
                )
            y = ring.tile([P, HALF], F32, name="y", bufs=4)
            nc.scalar.copy(y[:], y_bank[:])
            entries = idx3[:, half * HALF // LIST:(half + 1) * HALF // LIST]
            nc.vector.tensor_tensor(
                pages[n][:].indirect(entries), y[:], gate[:, half * HALF:(half + 1) * HALF], MULT
            )

        def hidden_half(half):
            per_half = HALF // CUES
            return [hidden(b, half, [damping(b, half * per_half + q) for q in range(per_half)]) for b in range(2)]

        h0 = hidden_half(0)
        for n in range(3):
            place(0, n, h0)
        h1 = hidden_half(1)
        place(0, 3, h0)
        for n in range(N // P):
            place(1, n, h1)
            nc.sync.dma_start(out[n * P:(n + 1) * P, :], pages[n][:])
